import numpy as np
import ml_dtypes


def mxq(x, axis, fmt="e4m3"):
    dtype, down = {"e4m3": (ml_dtypes.float8_e4m3fn, 7), "e5m2": (ml_dtypes.float8_e5m2, 14)}[fmt]
    v = np.moveaxis(np.asarray(x, np.float32).astype(ml_dtypes.bfloat16).astype(np.float64), axis, -1)
    blocks = v.reshape(v.shape[:-1] + (-1, 32))
    amax = np.abs(blocks).max(-1, keepdims=True)
    byte = np.maximum(np.where(amax > 0, np.frexp(amax)[1] - 1 + 127, 0) - down, 1)
    scale = np.exp2(byte - 127.0)
    codes = (blocks / scale).astype(np.float32).astype(dtype).astype(np.float64)
    return np.moveaxis((codes * scale).reshape(v.shape), -1, axis)


WIDE = False


def mx_kscale(k, group=512):
    if not WIDE:
        return np.ones(k)
    levels = np.array([18, -18])
    if group != 512:
        return np.exp2(np.random.permutation(np.resize(levels, k // group))).repeat(group)
    if k % 512:
        return np.exp2(np.random.permutation(np.resize(levels, k // 32))).repeat(32)
    a = np.empty((k // 512, 16))
    for p in range(k // 512):
        a[p, :8] = np.random.permutation(np.resize(levels, 8))
        for g in range(8):
            far = levels[np.abs(levels - a[p, g]) >= 10]
            a[p, g + 8] = far[np.random.randint(len(far))]
    return np.exp2(a.ravel()).repeat(32)


def f64(x):
    return np.asarray(x).astype(np.float64)


G, D, M, O, N = 4, 128, 128, 128, 512


def setup_inputs():
    n = np.random.standard_normal
    s_d = mx_kscale(D, 0)
    s_o = mx_kscale(O, 0)
    return {
        "x": (n((G, D, N)) * s_d[:, None]).astype(np.float32),
        "w1": (n((G, D, M)) / np.sqrt(D) / s_d[:, None]).astype(np.float32),
        "w2": (n((G, D, M)) / np.sqrt(D) / s_d[:, None]).astype(np.float32),
        "wo": (n((G, O, M)) / np.sqrt(O) / s_o[:, None]).astype(np.float32),
        "dy": (n((G, O, N)) * s_o[:, None]).astype(np.float32),
        "old": (0.3 * n((G, M, N))).astype(np.float32),
    }


def reference(x, w1, w2, wo, dy, old):
    w1q = mxq(f64(w1), 1, "e4m3")
    xq = mxq(f64(x), 1, "e4m3")
    z1 = w1q.transpose(0, 2, 1) @ xq
    w2q = mxq(f64(w2), 1, "e4m3")
    z2 = w2q.transpose(0, 2, 1) @ xq
    pr = z1 * z2
    mu = np.mean(pr, axis=-1, keepdims=True)
    ms = np.sqrt(np.mean(np.square(z1), axis=-1, keepdims=True) + 0.1)
    woq = mxq(f64(wo), 1, "e4m3")
    dyq = mxq(f64(dy), 1, "e4m3")
    c0 = woq.transpose(0, 2, 1) @ dyq
    dms = np.sum(c0 * (pr - mu) / np.square(ms) * (-1.0), axis=-1, keepdims=True)
    dmu = np.sum(c0 / ms * (-1.0), axis=-1, keepdims=True)
    dpr = c0 / ms + dmu / 512.0
    dz1 = dms * 0.5 / np.sqrt(np.mean(np.square(z1), axis=-1, keepdims=True) + 0.1) / 512.0 * z1 * 2.0 + dpr * z2
    y = dz1 + f64(old)
    return y

@@ -1,0 +1,185 @@
+from contextlib import ExitStack
+
+import concourse.mybir as mybir
+
+G, D, M, N = 4, 128, 128, 512
+FLOPS = 3 * 2 * G * D * M * N
+
+F32 = mybir.dt.float32
+BF16 = mybir.dt.bfloat16
+U32 = mybir.dt.uint32
+U8 = mybir.dt.uint8
+FP8X4 = mybir.dt.float8_e4m3fn_x4
+ACT = mybir.ActivationFunctionType
+ALU = mybir.AluOpType
+
+P = 128
+PACK = 4
+ROWS = D // PACK
+HALF = P // 2
+EPS = 0.1
+VECTOR_COLS = 352
+
+
+def tile_rows_browcorr_kernel(tc, x, w1, w2, wo, dy, old, out):
+    nc = tc.nc
+    with ExitStack() as ctx:
+        pool = ctx.enter_context(tc.tile_pool(name="sbuf", bufs=1))
+        psum = ctx.enter_context(tc.psum_pool(name="psum", bufs=1))
+        ctx.enter_context(tc.manual_schedule())
+
+        def sbuf(name, shape, dtype):
+            return pool.tile(shape, dtype, name=name, align_bytes=64)
+
+        def operand(name, width):
+            return {
+                "raw": sbuf(name + "_raw", [P, PACK, width], F32),
+                "bf16": sbuf(name + "_bf16", [P, width, PACK], BF16),
+                "codes": sbuf(name + "_codes", [P, width], U32),
+                "scales": sbuf(name + "_scales", [P, width], U8),
+            }
+
+        def load(op, low, high):
+            packed = "g (p j) c -> (g p) j c"
+            nc.sync.dma_start(out=op["raw"][:HALF], in_=low.rearrange(packed, j=PACK))
+            nc.scalar.dma_start(out=op["raw"][HALF:], in_=high.rearrange(packed, j=PACK))
+
+        def interleave(copy, op, cols):
+            copy(
+                out=op["bf16"][:, cols, :].rearrange("p (c i) j -> p c j i", i=4),
+                in_=op["raw"][:, :, cols].rearrange("p j (c i) -> p c j i", i=4),
+            )
+
+        def quantize(op):
+            nc.vector.quantize_mx(
+                out=op["codes"][:].bitcast(FP8X4),
+                scales=op["scales"][:],
+                in_=op["bf16"][:].rearrange("p c j -> p (c j)"),
+            )
+
+        def product(bank, tile, weights, data):
+            rows = slice(ROWS * tile, ROWS * (tile + 1))
+            nc.tensor.matmul_mx(
+                out=bank[:],
+                lhsT=weights["codes"][rows, :].bitcast(FP8X4),
+                lhsT_scale=weights["scales"][rows, :],
+                rhs=data["codes"][rows, :].bitcast(FP8X4),
+                rhs_scale=data["scales"][rows, :],
+                start=True,
+                stop=True,
+            )
+
+        first, second = slice(0, 2), slice(2, 4)
+        data_a, data_b = operand("data_a", N), operand("data_b", N)
+        weights_0, weights_1, weights_2 = [operand("weights_%d" % i, M) for i in range(3)]
+        z1 = [psum.tile([M, N], F32, name="z1_%d" % r) for r in range(G)]
+        shared = [psum.tile([M, N], F32, name="shared_%d" % r) for r in range(G)]
+
+        def stat(name):
+            return [sbuf("%s_%d" % (name, g), [M, 1], F32) for g in range(G)]
+
+        def full(name):
+            return [sbuf("%s_%d" % (name, g), [M, N], F32) for g in range(G)]
+
+        mean_sq, inv_ms, c_sum, c_mean, z1_factor, z1_coef = [
+            stat(name) for name in ("mean_sq", "inv_ms", "c_sum", "c_mean", "z1_factor", "z1_coef")
+        ]
+        squares, c_scaled, term, term_z1, partial, result = [
+            full(name) for name in ("squares", "c_scaled", "term", "term_z1", "partial", "result")
+        ]
+        old_sb = [sbuf("old_%d" % h, [M, 2, N], F32) for h in range(2)]
+        row_length = sbuf("row_length", [P, 1], F32)
+        inv_root_n = sbuf("inv_root_n", [P, 1], F32)
+
+        nc.vector.memset(row_length[:], float(N))
+        load(data_a, x[first], dy[first])
+        load(weights_0, w1[first], wo[first])
+        load(weights_1, w2[first], w1[second])
+        load(data_b, dy[second], x[second])
+        nc.scalar.activation(out=inv_root_n[:], in_=row_length[:], func=ACT.Abs_reciprocal_sqrt)
+        load(weights_2, wo[second], w2[second])
+        for h in range(2):
+            nc.sync.dma_start(out=old_sb[h][:], in_=old[2 * h : 2 * h + 2].rearrange("g m n -> m g n"))
+
+        def c_bank(g):
+            return shared[(g + 2) % G]
+
+        def scale_rows(g):
+            nc.scalar.activation(
+                out=squares[g][:], in_=z1[g][:], func=ACT.Square, scale=inv_root_n[:], accum_out=mean_sq[g][:]
+            )
+            nc.scalar.activation(out=inv_ms[g][:], in_=mean_sq[g][:], func=ACT.Abs_reciprocal_sqrt, bias=EPS)
+
+        def take_c(g):
+            nc.scalar.activation(
+                out=c_scaled[g][:], in_=c_bank(g)[:], func=ACT.Copy, scale=inv_ms[g][:], accum_out=c_sum[g][:]
+            )
+            nc.scalar.activation(out=c_mean[g][:], in_=c_sum[g][:], func=ACT.Copy, scale=1.0 / N)
+
+        def make_term(g):
+            nc.vector.scalar_tensor_tensor(
+                out=term[g][:], in0=c_scaled[g][:], scalar=c_mean[g][:], in1=shared[g][:],
+                op0=ALU.subtract, op1=ALU.mult,
+            )
+            nc.gpsimd.tensor_scalar(
+                out=z1_factor[g][:], in0=inv_ms[g][:], scalar1=inv_ms[g][:], scalar2=-1.0 / N,
+                op0=ALU.mult, op1=ALU.mult,
+            )
+            nc.gpsimd.tensor_tensor(out=partial[g][:], in0=term[g][:], in1=old_sb[g // 2][:, g % 2, :], op=ALU.add)
+
+        def make_coef(g):
+            nc.vector.scalar_tensor_tensor(
+                out=term_z1[g][:], in0=z1[g][:], scalar=z1_factor[g][:], in1=term[g][:],
+                op0=ALU.mult, op1=ALU.mult, accum_out=z1_coef[g][:],
+            )
+
+        def finish(g):
+            nc.vector.scalar_tensor_tensor(
+                out=result[g][:], in0=z1[g][:], scalar=z1_coef[g][:], in1=partial[g][:],
+                op0=ALU.mult, op1=ALU.add,
+            )
+            nc.sync.dma_start(out=out[g], in_=result[g][:])
+
+        every = slice(None)
+        interleave(nc.vector.tensor_copy, data_a, slice(0, VECTOR_COLS))
+        interleave(nc.scalar.copy, data_a, slice(VECTOR_COLS, N))
+        interleave(nc.scalar.copy, weights_0, every)
+        quantize(data_a)
+        interleave(nc.vector.tensor_copy, weights_1, every)
+        quantize(weights_0)
+        for g in (0, 1):
+            product(z1[g], g, weights_0, data_a)
+            product(c_bank(g), g + 2, weights_0, data_a)
+        quantize(weights_1)
+        for g in (0, 1):
+            product(shared[g], g, weights_1, data_a)
+
+        scale_rows(0)
+        take_c(0)
+        interleave(nc.vector.tensor_copy, data_b, every)
+        scale_rows(1)
+        take_c(1)
+        quantize(data_b)
+        for g in (2, 3):
+            product(z1[g], g, weights_1, data_b)
+        interleave(nc.scalar.copy, weights_2, every)
+        make_term(0)
+        make_term(1)
+        quantize(weights_2)
+        for g in (2, 3):
+            product(c_bank(g), g - 2, weights_2, data_b)
+            product(shared[g], g, weights_2, data_b)
+        scale_rows(2)
+        take_c(2)
+        scale_rows(3)
+        take_c(3)
+        make_coef(0)
+        make_coef(1)
+        finish(0)
+        make_term(2)
+        finish(1)
+        make_term(3)
+        make_coef(2)
+        make_coef(3)
+        finish(2)
+        finish(3)

@@ -16,7 +16,6 @@ ALU = mybir.AluOpType
 P = 128
 PACK = 4
 ROWS = D // PACK
-HALF = P // 2
 EPS = 0.1
 VECTOR_COLS = 352
 
@@ -31,18 +30,16 @@ def tile_rows_browcorr_kernel(tc, x, w1, w2, wo, dy, old, out):
         def sbuf(name, shape, dtype):
             return pool.tile(shape, dtype, name=name, align_bytes=64)
 
-        def operand(name, width):
-            return {
+        def load_operand(name, source):
+            width = source.shape[2]
+            op = {
                 "raw": sbuf(name + "_raw", [P, PACK, width], F32),
                 "bf16": sbuf(name + "_bf16", [P, width, PACK], BF16),
                 "codes": sbuf(name + "_codes", [P, width], U32),
                 "scales": sbuf(name + "_scales", [P, width], U8),
             }
-
-        def load(op, low, high):
-            packed = "g (p j) c -> (g p) j c"
-            nc.sync.dma_start(out=op["raw"][:HALF], in_=low.rearrange(packed, j=PACK))
-            nc.scalar.dma_start(out=op["raw"][HALF:], in_=high.rearrange(packed, j=PACK))
+            nc.sync.dma_start(out=op["raw"][:], in_=source.rearrange("g (p j) c -> (g p) j c", j=PACK))
+            return op
 
         def interleave(copy, op, cols):
             copy(
@@ -57,8 +54,8 @@ def tile_rows_browcorr_kernel(tc, x, w1, w2, wo, dy, old, out):
                 in_=op["bf16"][:].rearrange("p c j -> p (c j)"),
             )
 
-        def product(bank, tile, weights, data):
-            rows = slice(ROWS * tile, ROWS * (tile + 1))
+        def product(bank, g, weights, data):
+            rows = slice(ROWS * g, ROWS * (g + 1))
             nc.tensor.matmul_mx(
                 out=bank[:],
                 lhsT=weights["codes"][rows, :].bitcast(FP8X4),
@@ -69,67 +66,65 @@ def tile_rows_browcorr_kernel(tc, x, w1, w2, wo, dy, old, out):
                 stop=True,
             )
 
-        first, second = slice(0, 2), slice(2, 4)
-        data_a, data_b = operand("data_a", N), operand("data_b", N)
-        weights_0, weights_1, weights_2 = [operand("weights_%d" % i, M) for i in range(3)]
-        z1 = [psum.tile([M, N], F32, name="z1_%d" % r) for r in range(G)]
-        shared = [psum.tile([M, N], F32, name="shared_%d" % r) for r in range(G)]
+        z1 = [psum.tile([M, N], F32, name="z1_%d" % g) for g in range(G)]
+        c_then_z2 = [psum.tile([M, N], F32, name="c_then_z2_%d" % g) for g in range(G)]
 
-        def stat(name):
-            return [sbuf("%s_%d" % (name, g), [M, 1], F32) for g in range(G)]
+        def per_group(name, width):
+            return [sbuf("%s_%d" % (name, g), [M, width], F32) for g in range(G)]
 
-        def full(name):
-            return [sbuf("%s_%d" % (name, g), [M, N], F32) for g in range(G)]
-
-        mean_sq, inv_ms, c_sum, c_mean, z1_factor, z1_coef = [
-            stat(name) for name in ("mean_sq", "inv_ms", "c_sum", "c_mean", "z1_factor", "z1_coef")
-        ]
+        mean_sq, c_sum, c_mean, z1_coef = [per_group(name, 1) for name in ("mean_sq", "c_sum", "c_mean", "z1_coef")]
         squares, c_scaled, term, term_z1, partial, result = [
-            full(name) for name in ("squares", "c_scaled", "term", "term_z1", "partial", "result")
+            per_group(name, N) for name in ("squares", "c_scaled", "term", "term_z1", "partial", "result")
         ]
-        old_sb = [sbuf("old_%d" % h, [M, 2, N], F32) for h in range(2)]
+        inv_ms = sbuf("inv_ms", [M, G], F32)
+        z1_factor = sbuf("z1_factor", [M, G], F32)
         row_length = sbuf("row_length", [P, 1], F32)
         inv_root_n = sbuf("inv_root_n", [P, 1], F32)
 
-        nc.vector.memset(row_length[:], float(N))
-        load(data_a, x[first], dy[first])
-        load(weights_0, w1[first], wo[first])
-        load(weights_1, w2[first], w1[second])
-        load(data_b, dy[second], x[second])
-        nc.scalar.activation(out=inv_root_n[:], in_=row_length[:], func=ACT.Abs_reciprocal_sqrt)
-        load(weights_2, wo[second], w2[second])
+        x_op = load_operand("x", x)
+        w1_op = load_operand("w1", w1)
+        wo_op = load_operand("wo", wo)
+        dy_op = load_operand("dy", dy)
+        w2_op = load_operand("w2", w2)
+        old_sb = [sbuf("old_%d" % h, [M, 2, N], F32) for h in range(2)]
         for h in range(2):
             nc.sync.dma_start(out=old_sb[h][:], in_=old[2 * h : 2 * h + 2].rearrange("g m n -> m g n"))
 
-        def c_bank(g):
-            return shared[(g + 2) % G]
+        nc.vector.memset(row_length[:], float(N))
+        nc.scalar.activation(out=inv_root_n[:], in_=row_length[:], func=ACT.Abs_reciprocal_sqrt)
 
-        def scale_rows(g):
+        def row_scale(g):
             nc.scalar.activation(
                 out=squares[g][:], in_=z1[g][:], func=ACT.Square, scale=inv_root_n[:], accum_out=mean_sq[g][:]
             )
-            nc.scalar.activation(out=inv_ms[g][:], in_=mean_sq[g][:], func=ACT.Abs_reciprocal_sqrt, bias=EPS)
+            nc.scalar.activation(
+                out=inv_ms[:, g : g + 1], in_=mean_sq[g][:], func=ACT.Abs_reciprocal_sqrt, bias=EPS
+            )
 
         def take_c(g):
             nc.scalar.activation(
-                out=c_scaled[g][:], in_=c_bank(g)[:], func=ACT.Copy, scale=inv_ms[g][:], accum_out=c_sum[g][:]
+                out=c_scaled[g][:], in_=c_then_z2[g][:], func=ACT.Copy, scale=inv_ms[:, g : g + 1],
+                accum_out=c_sum[g][:],
             )
             nc.scalar.activation(out=c_mean[g][:], in_=c_sum[g][:], func=ACT.Copy, scale=1.0 / N)
+            product(c_then_z2[g], g, w2_op, x_op)
+
+        def make_factors(groups):
+            nc.vector.scalar_tensor_tensor(
+                out=z1_factor[:, groups], in0=inv_ms[:, groups], scalar=-1.0 / N, in1=inv_ms[:, groups],
+                op0=ALU.mult, op1=ALU.mult,
+            )
 
         def make_term(g):
             nc.vector.scalar_tensor_tensor(
-                out=term[g][:], in0=c_scaled[g][:], scalar=c_mean[g][:], in1=shared[g][:],
+                out=term[g][:], in0=c_scaled[g][:], scalar=c_mean[g][:], in1=c_then_z2[g][:],
                 op0=ALU.subtract, op1=ALU.mult,
-            )
-            nc.gpsimd.tensor_scalar(
-                out=z1_factor[g][:], in0=inv_ms[g][:], scalar1=inv_ms[g][:], scalar2=-1.0 / N,
-                op0=ALU.mult, op1=ALU.mult,
             )
             nc.gpsimd.tensor_tensor(out=partial[g][:], in0=term[g][:], in1=old_sb[g // 2][:, g % 2, :], op=ALU.add)
 
         def make_coef(g):
             nc.vector.scalar_tensor_tensor(
-                out=term_z1[g][:], in0=z1[g][:], scalar=z1_factor[g][:], in1=term[g][:],
+                out=term_z1[g][:], in0=z1[g][:], scalar=z1_factor[:, g : g + 1], in1=term[g][:],
                 op0=ALU.mult, op1=ALU.mult, accum_out=z1_coef[g][:],
             )
 
@@ -141,45 +136,44 @@ def tile_rows_browcorr_kernel(tc, x, w1, w2, wo, dy, old, out):
             nc.sync.dma_start(out=out[g], in_=result[g][:])
 
         every = slice(None)
-        interleave(nc.vector.tensor_copy, data_a, slice(0, VECTOR_COLS))
-        interleave(nc.scalar.copy, data_a, slice(VECTOR_COLS, N))
-        interleave(nc.scalar.copy, weights_0, every)
-        quantize(data_a)
-        interleave(nc.vector.tensor_copy, weights_1, every)
-        quantize(weights_0)
-        for g in (0, 1):
-            product(z1[g], g, weights_0, data_a)
-            product(c_bank(g), g + 2, weights_0, data_a)
-        quantize(weights_1)
-        for g in (0, 1):
-            product(shared[g], g, weights_1, data_a)
+        interleave(nc.vector.tensor_copy, x_op, slice(0, VECTOR_COLS))
+        interleave(nc.scalar.copy, x_op, slice(VECTOR_COLS, N))
+        interleave(nc.scalar.copy, w1_op, every)
+        quantize(x_op)
+        interleave(nc.vector.tensor_copy, wo_op, every)
+        quantize(w1_op)
+        for g in range(G):
+            product(z1[g], g, w1_op, x_op)
+        quantize(wo_op)
+        row_scale(0)
 
-        scale_rows(0)
+        interleave(nc.vector.tensor_copy, dy_op, slice(0, VECTOR_COLS))
+        interleave(nc.scalar.copy, dy_op, slice(VECTOR_COLS, N))
+        row_scale(1)
+        quantize(dy_op)
+        for g in range(G):
+            product(c_then_z2[g], g, wo_op, dy_op)
+        interleave(nc.vector.tensor_copy, w2_op, every)
+        make_factors(slice(0, 2))
+        quantize(w2_op)
+
         take_c(0)
-        interleave(nc.vector.tensor_copy, data_b, every)
-        scale_rows(1)
         take_c(1)
-        quantize(data_b)
-        for g in (2, 3):
-            product(z1[g], g, weights_1, data_b)
-        interleave(nc.scalar.copy, weights_2, every)
-        make_term(0)
-        make_term(1)
-        quantize(weights_2)
-        for g in (2, 3):
-            product(c_bank(g), g - 2, weights_2, data_b)
-            product(shared[g], g, weights_2, data_b)
-        scale_rows(2)
+        row_scale(2)
         take_c(2)
-        scale_rows(3)
+        row_scale(3)
         take_c(3)
+
+        make_term(0)
         make_coef(0)
+        make_term(1)
         make_coef(1)
-        finish(0)
         make_term(2)
-        finish(1)
-        make_term(3)
+        finish(0)
+        make_factors(slice(2, 4))
         make_coef(2)
+        make_term(3)
+        finish(1)
         make_coef(3)
         finish(2)
         finish(3)

@@ -17,7 +17,7 @@ P = 128
 PACK = 4
 ROWS = D // PACK
 EPS = 0.1
-VECTOR_COLS = 352
+VECTOR_COLS = 320
 
 
 def tile_rows_browcorr_kernel(tc, x, w1, w2, wo, dy, old, out):
@@ -43,16 +43,24 @@ def tile_rows_browcorr_kernel(tc, x, w1, w2, wo, dy, old, out):
 
         def interleave(copy, op, cols):
             copy(
-                out=op["bf16"][:, cols, :].rearrange("p (c i) j -> p c j i", i=4),
-                in_=op["raw"][:, :, cols].rearrange("p j (c i) -> p c j i", i=4),
+                out=op["bf16"][:, cols, :].rearrange("p (c i) j -> p c j i", i=2),
+                in_=op["raw"][:, :, cols].rearrange("p j (c i) -> p c j i", i=2),
             )
 
-        def quantize(op):
+        def quantize(op, cols):
             nc.vector.quantize_mx(
-                out=op["codes"][:].bitcast(FP8X4),
-                scales=op["scales"][:],
-                in_=op["bf16"][:].rearrange("p c j -> p (c j)"),
+                out=op["codes"][:, cols].bitcast(FP8X4),
+                scales=op["scales"][:, cols],
+                in_=op["bf16"][:, cols, :].rearrange("p c j -> p (c j)"),
             )
+
+        def prepare_wide(op):
+            low, high = slice(0, N // 2), slice(N // 2, N)
+            interleave(nc.vector.tensor_copy, op, low)
+            interleave(nc.vector.tensor_copy, op, slice(N // 2, VECTOR_COLS))
+            interleave(nc.scalar.copy, op, slice(VECTOR_COLS, N))
+            quantize(op, low)
+            quantize(op, high)
 
         def product(bank, g, weights, data):
             rows = slice(ROWS * g, ROWS * (g + 1))
@@ -66,18 +74,21 @@ def tile_rows_browcorr_kernel(tc, x, w1, w2, wo, dy, old, out):
                 stop=True,
             )
 
-        z1 = [psum.tile([M, N], F32, name="z1_%d" % g) for g in range(G)]
-        c_then_z2 = [psum.tile([M, N], F32, name="c_then_z2_%d" % g) for g in range(G)]
+        first_z1 = [psum.tile([M, N], F32, name="first_z1_%d" % g) for g in range(G)]
+        c_bank = [psum.tile([M, N], F32, name="c_bank_%d" % g) for g in range(G)]
+        z1 = c_bank[:1] + first_z1[1:]
+        z2 = first_z1[:1] + c_bank[1:]
 
         def per_group(name, width):
             return [sbuf("%s_%d" % (name, g), [M, width], F32) for g in range(G)]
 
-        mean_sq, c_sum, c_mean, z1_coef = [per_group(name, 1) for name in ("mean_sq", "c_sum", "c_mean", "z1_coef")]
+        mean_sq, coef_sum, z1_coef = [per_group(name, 1) for name in ("mean_sq", "coef_sum", "z1_coef")]
+        row_stats, neg_over_n = [per_group(name, 2) for name in ("row_stats", "neg_over_n")]
         squares, c_scaled, term, term_z1, partial, result = [
             per_group(name, N) for name in ("squares", "c_scaled", "term", "term_z1", "partial", "result")
         ]
-        inv_ms = sbuf("inv_ms", [M, G], F32)
-        z1_factor = sbuf("z1_factor", [M, G], F32)
+        inv_ms = [stats[:, 0:1] for stats in row_stats]
+        c_sum = [stats[:, 1:2] for stats in row_stats]
         row_length = sbuf("row_length", [P, 1], F32)
         inv_root_n = sbuf("inv_root_n", [P, 1], F32)
 
@@ -93,87 +104,108 @@ def tile_rows_browcorr_kernel(tc, x, w1, w2, wo, dy, old, out):
         nc.vector.memset(row_length[:], float(N))
         nc.scalar.activation(out=inv_root_n[:], in_=row_length[:], func=ACT.Abs_reciprocal_sqrt)
 
+        def sum_squares(g):
+            nc.scalar.activation(
+                out=squares[g][:], in_=first_z1[g][:], func=ACT.Square, scale=inv_root_n[:],
+                accum_out=mean_sq[g][:],
+            )
+
         def row_scale(g):
-            nc.scalar.activation(
-                out=squares[g][:], in_=z1[g][:], func=ACT.Square, scale=inv_root_n[:], accum_out=mean_sq[g][:]
-            )
-            nc.scalar.activation(
-                out=inv_ms[:, g : g + 1], in_=mean_sq[g][:], func=ACT.Abs_reciprocal_sqrt, bias=EPS
-            )
+            nc.scalar.activation(out=inv_ms[g], in_=mean_sq[g][:], func=ACT.Abs_reciprocal_sqrt, bias=EPS)
 
-        def take_c(g):
+        def take_c_on_scalar(g):
             nc.scalar.activation(
-                out=c_scaled[g][:], in_=c_then_z2[g][:], func=ACT.Copy, scale=inv_ms[:, g : g + 1],
-                accum_out=c_sum[g][:],
+                out=c_scaled[g][:], in_=c_bank[g][:], func=ACT.Copy, scale=inv_ms[g], accum_out=c_sum[g]
             )
-            nc.scalar.activation(out=c_mean[g][:], in_=c_sum[g][:], func=ACT.Copy, scale=1.0 / N)
-            product(c_then_z2[g], g, w2_op, x_op)
+            product(z2[g], g, w2_op, x_op)
 
-        def make_factors(groups):
-            nc.vector.scalar_tensor_tensor(
-                out=z1_factor[:, groups], in0=inv_ms[:, groups], scalar=-1.0 / N, in1=inv_ms[:, groups],
-                op0=ALU.mult, op1=ALU.mult,
+        def take_c_on_vector(g):
+            nc.vector.tensor_scalar(
+                out=c_scaled[g][:], in0=c_bank[g][:], scalar1=inv_ms[g], scalar2=None,
+                op0=ALU.mult, op1=ALU.add, accum_out=c_sum[g],
+            )
+            product(z1[g], g, w1_op, x_op)
+
+        def divide_stats(g):
+            nc.scalar.activation(out=neg_over_n[g][:], in_=row_stats[g][:], func=ACT.Copy, scale=-1.0 / N)
+
+        def divide_stats_on_vector(g):
+            nc.vector.tensor_scalar(
+                out=neg_over_n[g][:], in0=row_stats[g][:], scalar1=-1.0 / N, scalar2=None, op0=ALU.mult
             )
 
         def make_term(g):
             nc.vector.scalar_tensor_tensor(
-                out=term[g][:], in0=c_scaled[g][:], scalar=c_mean[g][:], in1=c_then_z2[g][:],
-                op0=ALU.subtract, op1=ALU.mult,
+                out=term[g][:], in0=c_scaled[g][:], scalar=neg_over_n[g][:, 1:2], in1=z2[g][:],
+                op0=ALU.add, op1=ALU.mult,
             )
             nc.gpsimd.tensor_tensor(out=partial[g][:], in0=term[g][:], in1=old_sb[g // 2][:, g % 2, :], op=ALU.add)
 
         def make_coef(g):
             nc.vector.scalar_tensor_tensor(
-                out=term_z1[g][:], in0=z1[g][:], scalar=z1_factor[:, g : g + 1], in1=term[g][:],
-                op0=ALU.mult, op1=ALU.mult, accum_out=z1_coef[g][:],
+                out=term_z1[g][:], in0=z1[g][:], scalar=neg_over_n[g][:, 0:1], in1=term[g][:],
+                op0=ALU.mult, op1=ALU.mult, accum_out=coef_sum[g][:],
             )
 
-        def finish(g):
+        def scale_coef(g):
+            nc.scalar.activation(out=z1_coef[g][:], in_=coef_sum[g][:], func=ACT.Copy, scale=inv_ms[g])
+
+        def finish(g, cols, queue):
             nc.vector.scalar_tensor_tensor(
-                out=result[g][:], in0=z1[g][:], scalar=z1_coef[g][:], in1=partial[g][:],
+                out=result[g][:, cols], in0=z1[g][:, cols], scalar=z1_coef[g][:], in1=partial[g][:, cols],
                 op0=ALU.mult, op1=ALU.add,
             )
-            nc.sync.dma_start(out=out[g], in_=result[g][:])
+            queue.dma_start(out=out[g][:, cols], in_=result[g][:, cols])
 
         every = slice(None)
-        interleave(nc.vector.tensor_copy, x_op, slice(0, VECTOR_COLS))
-        interleave(nc.scalar.copy, x_op, slice(VECTOR_COLS, N))
+        prepare_wide(x_op)
         interleave(nc.scalar.copy, w1_op, every)
-        quantize(x_op)
+        quantize(w1_op, every)
+        for g in range(G):
+            product(first_z1[g], g, w1_op, x_op)
         interleave(nc.vector.tensor_copy, wo_op, every)
-        quantize(w1_op)
-        for g in range(G):
-            product(z1[g], g, w1_op, x_op)
-        quantize(wo_op)
+        quantize(wo_op, every)
+        sum_squares(0)
+
+        prepare_wide(dy_op)
+        for g in (0, 1):
+            product(c_bank[g], g, wo_op, dy_op)
         row_scale(0)
-
-        interleave(nc.vector.tensor_copy, dy_op, slice(0, VECTOR_COLS))
-        interleave(nc.scalar.copy, dy_op, slice(VECTOR_COLS, N))
+        sum_squares(1)
+        sum_squares(2)
         row_scale(1)
-        quantize(dy_op)
-        for g in range(G):
-            product(c_then_z2[g], g, wo_op, dy_op)
-        interleave(nc.vector.tensor_copy, w2_op, every)
-        make_factors(slice(0, 2))
-        quantize(w2_op)
-
-        take_c(0)
-        take_c(1)
         row_scale(2)
-        take_c(2)
+        interleave(nc.vector.tensor_copy, w2_op, every)
+        quantize(w2_op, every)
+        product(z2[0], 0, w2_op, x_op)
+        product(c_bank[2], 2, wo_op, dy_op)
+
+        take_c_on_vector(0)
+        divide_stats_on_vector(0)
+        take_c_on_scalar(1)
+        product(c_bank[3], 3, wo_op, dy_op)
+        take_c_on_scalar(2)
+        divide_stats(1)
+        sum_squares(3)
+        divide_stats(2)
         row_scale(3)
-        take_c(3)
+        take_c_on_scalar(3)
 
         make_term(0)
         make_coef(0)
+        scale_coef(0)
+        divide_stats(3)
         make_term(1)
-        make_coef(1)
         make_term(2)
-        finish(0)
-        make_factors(slice(2, 4))
-        make_coef(2)
+        make_coef(1)
+        scale_coef(1)
+        finish(0, every, nc.sync)
         make_term(3)
-        finish(1)
+        make_coef(2)
+        scale_coef(2)
+        finish(1, every, nc.sync)
         make_coef(3)
-        finish(2)
-        finish(3)
+        scale_coef(3)
+        finish(2, every, nc.sync)
+        finish(3, slice(0, N // 2), nc.sync)
+        finish(3, slice(N // 2, N), nc.scalar)

@@ -30,21 +30,22 @@ def tile_rows_browcorr_kernel(tc, x, w1, w2, wo, dy, old, out):
         def sbuf(name, shape, dtype):
             return pool.tile(shape, dtype, name=name, align_bytes=64)
 
-        def load_operand(name, source):
-            width = source.shape[2]
-            op = {
-                "raw": sbuf(name + "_raw", [P, PACK, width], F32),
+        def load_raw(name, source):
+            raw = sbuf(name + "_raw", [P, PACK, source.shape[2]], F32)
+            nc.sync.dma_start(out=raw[:], in_=source.rearrange("g (p j) c -> (g p) j c", j=PACK))
+            return raw
+
+        def operand(name, width):
+            return {
                 "bf16": sbuf(name + "_bf16", [P, width, PACK], BF16),
                 "codes": sbuf(name + "_codes", [P, width], U32),
                 "scales": sbuf(name + "_scales", [P, width], U8),
             }
-            nc.sync.dma_start(out=op["raw"][:], in_=source.rearrange("g (p j) c -> (g p) j c", j=PACK))
-            return op
 
-        def interleave(copy, op, cols):
+        def interleave(copy, op, cols, raw):
             copy(
                 out=op["bf16"][:, cols, :].rearrange("p (c i) j -> p c j i", i=2),
-                in_=op["raw"][:, :, cols].rearrange("p j (c i) -> p c j i", i=2),
+                in_=raw.rearrange("p j (c i) -> p c j i", i=2),
             )
 
         def quantize(op, cols):
@@ -54,13 +55,6 @@ def tile_rows_browcorr_kernel(tc, x, w1, w2, wo, dy, old, out):
                 in_=op["bf16"][:, cols, :].rearrange("p c j -> p (c j)"),
             )
 
-        def prepare_wide(op):
-            low, high = slice(0, N // 2), slice(N // 2, N)
-            interleave(nc.vector.tensor_copy, op, low)
-            interleave(nc.vector.tensor_copy, op, slice(N // 2, VECTOR_COLS))
-            interleave(nc.scalar.copy, op, slice(VECTOR_COLS, N))
-            quantize(op, low)
-            quantize(op, high)
 
         def product(bank, g, weights, data):
             rows = slice(ROWS * g, ROWS * (g + 1))
@@ -92,11 +86,15 @@ def tile_rows_browcorr_kernel(tc, x, w1, w2, wo, dy, old, out):
         row_length = sbuf("row_length", [P, 1], F32)
         inv_root_n = sbuf("inv_root_n", [P, 1], F32)
 
-        x_op = load_operand("x", x)
-        w1_op = load_operand("w1", w1)
-        wo_op = load_operand("wo", wo)
-        dy_op = load_operand("dy", dy)
-        w2_op = load_operand("w2", w2)
+        low, high, every = slice(0, N // 2), slice(N // 2, N), slice(None)
+        x_op, dy_op = operand("x", N), operand("dy", N)
+        w1_op, w2_op, wo_op = operand("w1", M), operand("w2", M), operand("wo", M)
+        x_raw = load_raw("x", x)
+        w1_raw = load_raw("w1", w1)
+        dy_low_raw = load_raw("dy_low", dy[:, :, low])
+        dy_high_raw = load_raw("dy_high", dy[:, :, high])
+        wo_raw = load_raw("wo", wo)
+        w2_raw = load_raw("w2", w2)
         old_sb = [sbuf("old_%d" % h, [M, 2, N], F32) for h in range(2)]
         for h in range(2):
             nc.sync.dma_start(out=old_sb[h][:], in_=old[2 * h : 2 * h + 2].rearrange("g m n -> m g n"))
@@ -157,17 +155,25 @@ def tile_rows_browcorr_kernel(tc, x, w1, w2, wo, dy, old, out):
             )
             queue.dma_start(out=out[g][:, cols], in_=result[g][:, cols])
 
-        every = slice(None)
-        prepare_wide(x_op)
-        interleave(nc.scalar.copy, w1_op, every)
+        for copy, cols in (
+            (nc.vector.tensor_copy, low),
+            (nc.vector.tensor_copy, slice(N // 2, VECTOR_COLS)),
+            (nc.scalar.copy, slice(VECTOR_COLS, N)),
+        ):
+            interleave(copy, x_op, cols, x_raw[:, :, cols])
+        quantize(x_op, low)
+        quantize(x_op, high)
+        interleave(nc.scalar.copy, w1_op, every, w1_raw[:])
         quantize(w1_op, every)
         for g in range(G):
             product(first_z1[g], g, w1_op, x_op)
-        interleave(nc.vector.tensor_copy, wo_op, every)
-        quantize(wo_op, every)
         sum_squares(0)
 
-        prepare_wide(dy_op)
+        for cols, raw in ((low, dy_low_raw), (high, dy_high_raw)):
+            interleave(nc.vector.tensor_copy, dy_op, cols, raw[:])
+            quantize(dy_op, cols)
+        interleave(nc.scalar.copy, wo_op, every, wo_raw[:])
+        quantize(wo_op, every)
         for g in (0, 1):
             product(c_bank[g], g, wo_op, dy_op)
         row_scale(0)
@@ -175,7 +181,7 @@ def tile_rows_browcorr_kernel(tc, x, w1, w2, wo, dy, old, out):
         sum_squares(2)
         row_scale(1)
         row_scale(2)
-        interleave(nc.vector.tensor_copy, w2_op, every)
+        interleave(nc.vector.tensor_copy, w2_op, every, w2_raw[:])
         quantize(w2_op, every)
         product(z2[0], 0, w2_op, x_op)
         product(c_bank[2], 2, wo_op, dy_op)
@@ -200,12 +206,12 @@ def tile_rows_browcorr_kernel(tc, x, w1, w2, wo, dy, old, out):
         make_coef(1)
         scale_coef(1)
         finish(0, every, nc.sync)
-        make_term(3)
         make_coef(2)
         scale_coef(2)
+        make_term(3)
         finish(1, every, nc.sync)
         make_coef(3)
         scale_coef(3)
         finish(2, every, nc.sync)
-        finish(3, slice(0, N // 2), nc.sync)
-        finish(3, slice(N // 2, N), nc.scalar)
+        finish(3, low, nc.sync)
+        finish(3, high, nc.scalar)

from contextlib import ExitStack

import concourse.mybir as mybir

G, D, M, N = 4, 128, 128, 512
FLOPS = 3 * 2 * G * D * M * N

F32 = mybir.dt.float32
BF16 = mybir.dt.bfloat16
U32 = mybir.dt.uint32
U8 = mybir.dt.uint8
FP8X4 = mybir.dt.float8_e4m3fn_x4
ACT = mybir.ActivationFunctionType
ALU = mybir.AluOpType

P = 128
PACK = 4
ROWS = D // PACK
EPS = 0.1
VECTOR_COLS = 320


def tile_rows_browcorr_kernel(tc, x, w1, w2, wo, dy, old, out):
    nc = tc.nc
    with ExitStack() as ctx:
        pool = ctx.enter_context(tc.tile_pool(name="sbuf", bufs=1))
        psum = ctx.enter_context(tc.psum_pool(name="psum", bufs=1))
        ctx.enter_context(tc.manual_schedule())

        def sbuf(name, shape, dtype):
            return pool.tile(shape, dtype, name=name, align_bytes=64)

        def load_raw(name, source):
            raw = sbuf(name + "_raw", [P, PACK, source.shape[2]], F32)
            nc.sync.dma_start(out=raw[:], in_=source.rearrange("g (p j) c -> (g p) j c", j=PACK))
            return raw

        def operand(name, width):
            return {
                "bf16": sbuf(name + "_bf16", [P, width, PACK], BF16),
                "codes": sbuf(name + "_codes", [P, width], U32),
                "scales": sbuf(name + "_scales", [P, width], U8),
            }

        def interleave(copy, op, cols, raw):
            copy(
                out=op["bf16"][:, cols, :].rearrange("p (c i) j -> p c j i", i=2),
                in_=raw.rearrange("p j (c i) -> p c j i", i=2),
            )

        def quantize(op, cols):
            nc.vector.quantize_mx(
                out=op["codes"][:, cols].bitcast(FP8X4),
                scales=op["scales"][:, cols],
                in_=op["bf16"][:, cols, :].rearrange("p c j -> p (c j)"),
            )


        def product(bank, g, weights, data):
            rows = slice(ROWS * g, ROWS * (g + 1))
            nc.tensor.matmul_mx(
                out=bank[:],
                lhsT=weights["codes"][rows, :].bitcast(FP8X4),
                lhsT_scale=weights["scales"][rows, :],
                rhs=data["codes"][rows, :].bitcast(FP8X4),
                rhs_scale=data["scales"][rows, :],
                start=True,
                stop=True,
            )

        first_z1 = [psum.tile([M, N], F32, name="first_z1_%d" % g) for g in range(G)]
        c_bank = [psum.tile([M, N], F32, name="c_bank_%d" % g) for g in range(G)]
        z1 = c_bank[:1] + first_z1[1:]
        z2 = first_z1[:1] + c_bank[1:]

        def per_group(name, width):
            return [sbuf("%s_%d" % (name, g), [M, width], F32) for g in range(G)]

        mean_sq, coef_sum, z1_coef = [per_group(name, 1) for name in ("mean_sq", "coef_sum", "z1_coef")]
        row_stats, neg_over_n = [per_group(name, 2) for name in ("row_stats", "neg_over_n")]
        squares, c_scaled, term, term_z1, partial, result = [
            per_group(name, N) for name in ("squares", "c_scaled", "term", "term_z1", "partial", "result")
        ]
        inv_ms = [stats[:, 0:1] for stats in row_stats]
        c_sum = [stats[:, 1:2] for stats in row_stats]
        row_length = sbuf("row_length", [P, 1], F32)
        inv_root_n = sbuf("inv_root_n", [P, 1], F32)

        low, high, every = slice(0, N // 2), slice(N // 2, N), slice(None)
        x_op, dy_op = operand("x", N), operand("dy", N)
        w1_op, w2_op, wo_op = operand("w1", M), operand("w2", M), operand("wo", M)
        x_raw = load_raw("x", x)
        w1_raw = load_raw("w1", w1)
        dy_low_raw = load_raw("dy_low", dy[:, :, low])
        dy_high_raw = load_raw("dy_high", dy[:, :, high])
        wo_raw = load_raw("wo", wo)
        w2_raw = load_raw("w2", w2)
        old_sb = [sbuf("old_%d" % h, [M, 2, N], F32) for h in range(2)]
        for h in range(2):
            nc.sync.dma_start(out=old_sb[h][:], in_=old[2 * h : 2 * h + 2].rearrange("g m n -> m g n"))

        nc.vector.memset(row_length[:], float(N))
        nc.scalar.activation(out=inv_root_n[:], in_=row_length[:], func=ACT.Abs_reciprocal_sqrt)

        def sum_squares(g):
            nc.scalar.activation(
                out=squares[g][:], in_=first_z1[g][:], func=ACT.Square, scale=inv_root_n[:],
                accum_out=mean_sq[g][:],
            )

        def row_scale(g):
            nc.scalar.activation(out=inv_ms[g], in_=mean_sq[g][:], func=ACT.Abs_reciprocal_sqrt, bias=EPS)

        def take_c_on_scalar(g):
            nc.scalar.activation(
                out=c_scaled[g][:], in_=c_bank[g][:], func=ACT.Copy, scale=inv_ms[g], accum_out=c_sum[g]
            )
            product(z2[g], g, w2_op, x_op)

        def take_c_on_vector(g):
            nc.vector.tensor_scalar(
                out=c_scaled[g][:], in0=c_bank[g][:], scalar1=inv_ms[g], scalar2=None,
                op0=ALU.mult, op1=ALU.add, accum_out=c_sum[g],
            )
            product(z1[g], g, w1_op, x_op)

        def divide_stats(g):
            nc.scalar.activation(out=neg_over_n[g][:], in_=row_stats[g][:], func=ACT.Copy, scale=-1.0 / N)

        def divide_stats_on_vector(g):
            nc.vector.tensor_scalar(
                out=neg_over_n[g][:], in0=row_stats[g][:], scalar1=-1.0 / N, scalar2=None, op0=ALU.mult
            )

        def make_term(g):
            nc.vector.scalar_tensor_tensor(
                out=term[g][:], in0=c_scaled[g][:], scalar=neg_over_n[g][:, 1:2], in1=z2[g][:],
                op0=ALU.add, op1=ALU.mult,
            )
            nc.gpsimd.tensor_tensor(out=partial[g][:], in0=term[g][:], in1=old_sb[g // 2][:, g % 2, :], op=ALU.add)

        def make_coef(g):
            nc.vector.scalar_tensor_tensor(
                out=term_z1[g][:], in0=z1[g][:], scalar=neg_over_n[g][:, 0:1], in1=term[g][:],
                op0=ALU.mult, op1=ALU.mult, accum_out=coef_sum[g][:],
            )

        def scale_coef(g):
            nc.scalar.activation(out=z1_coef[g][:], in_=coef_sum[g][:], func=ACT.Copy, scale=inv_ms[g])

        def finish(g, cols, queue):
            nc.vector.scalar_tensor_tensor(
                out=result[g][:, cols], in0=z1[g][:, cols], scalar=z1_coef[g][:], in1=partial[g][:, cols],
                op0=ALU.mult, op1=ALU.add,
            )
            queue.dma_start(out=out[g][:, cols], in_=result[g][:, cols])

        for copy, cols in (
            (nc.vector.tensor_copy, low),
            (nc.vector.tensor_copy, slice(N // 2, VECTOR_COLS)),
            (nc.scalar.copy, slice(VECTOR_COLS, N)),
        ):
            interleave(copy, x_op, cols, x_raw[:, :, cols])
        quantize(x_op, low)
        quantize(x_op, high)
        interleave(nc.scalar.copy, w1_op, every, w1_raw[:])
        quantize(w1_op, every)
        for g in range(G):
            product(first_z1[g], g, w1_op, x_op)
        sum_squares(0)

        for cols, raw in ((low, dy_low_raw), (high, dy_high_raw)):
            interleave(nc.vector.tensor_copy, dy_op, cols, raw[:])
            quantize(dy_op, cols)
        interleave(nc.scalar.copy, wo_op, every, wo_raw[:])
        quantize(wo_op, every)
        for g in (0, 1):
            product(c_bank[g], g, wo_op, dy_op)
        row_scale(0)
        sum_squares(1)
        sum_squares(2)
        row_scale(1)
        row_scale(2)
        interleave(nc.vector.tensor_copy, w2_op, every, w2_raw[:])
        quantize(w2_op, every)
        product(z2[0], 0, w2_op, x_op)
        product(c_bank[2], 2, wo_op, dy_op)

        take_c_on_vector(0)
        divide_stats_on_vector(0)
        take_c_on_scalar(1)
        product(c_bank[3], 3, wo_op, dy_op)
        take_c_on_scalar(2)
        divide_stats(1)
        sum_squares(3)
        divide_stats(2)
        row_scale(3)
        take_c_on_scalar(3)

        make_term(0)
        make_coef(0)
        scale_coef(0)
        divide_stats(3)
        make_term(1)
        make_term(2)
        make_coef(1)
        scale_coef(1)
        finish(0, every, nc.sync)
        make_coef(2)
        scale_coef(2)
        make_term(3)
        finish(1, every, nc.sync)
        make_coef(3)
        scale_coef(3)
        finish(2, every, nc.sync)
        finish(3, low, nc.sync)
        finish(3, high, nc.scalar)
